import numpy as np
import ml_dtypes


def mxq(x, axis, fmt="e4m3"):
    dtype, down = {"e4m3": (ml_dtypes.float8_e4m3fn, 7), "e5m2": (ml_dtypes.float8_e5m2, 14)}[fmt]
    v = np.moveaxis(np.asarray(x, np.float32).astype(ml_dtypes.bfloat16).astype(np.float64), axis, -1)
    blocks = v.reshape(v.shape[:-1] + (-1, 32))
    amax = np.abs(blocks).max(-1, keepdims=True)
    byte = np.maximum(np.where(amax > 0, np.frexp(amax)[1] - 1 + 127, 0) - down, 1)
    scale = np.exp2(byte - 127.0)
    codes = (blocks / scale).astype(np.float32).astype(dtype).astype(np.float64)
    return np.moveaxis((codes * scale).reshape(v.shape), -1, axis)


WIDE = False


def mx_kscale(k):
    if not WIDE:
        return np.ones(k)
    levels = np.array([10, -10, 5, -5, 0])
    if k % 512:
        return np.exp2(np.random.permutation(np.resize(levels, k // 32))).repeat(32)
    a = np.empty((k // 512, 16))
    for p in range(k // 512):
        a[p, :8] = np.random.permutation(np.resize(levels, 8))
        for g in range(8):
            far = levels[np.abs(levels - a[p, g]) >= 10]
            a[p, g + 8] = far[np.random.randint(len(far))]
    return np.exp2(a.ravel()).repeat(32)


def f64(x):
    return np.asarray(x).astype(np.float64)


def striped(idx):
    return np.tile(idx.reshape(-1, 16).T, (8, 1)).astype(np.uint16)


def unstriped(offs):
    return offs[:16].T.reshape(-1).astype(np.int64)


def pack_weight(w):
    k, n = w.shape
    w = f64(np.asarray(w, np.float32).astype(ml_dtypes.bfloat16)).reshape(k // 32, 32, n)
    amax = np.abs(w).max(1)
    byte = np.clip(np.where(amax > 0, np.frexp(amax)[1] - 1 + 127 - 7, 1), 1, 254)
    scaled = (w * np.exp2(127.0 - byte)[:, None, :]).reshape(k, n).astype(np.float32)
    words = np.ascontiguousarray(scaled.reshape(k // 512, 128, 4, n).transpose(0, 1, 3, 2)).astype(ml_dtypes.float8_e4m3fn).view(np.uint8)
    return words, np.ascontiguousarray(byte.astype(np.uint8).reshape(k // 512, 16, n))


def unpack_weight(words, scales):
    g, p, n, _ = words.shape
    vals = np.ascontiguousarray(words).view(ml_dtypes.float8_e4m3fn).astype(np.float64) * np.repeat(np.exp2(scales.astype(np.float64) - 127.0), 8, axis=1)[..., None]
    return vals.transpose(0, 1, 3, 2).reshape(g * 512, n)


def planes(y):
    n, m = y.shape
    v = y.astype(np.float32).astype(ml_dtypes.bfloat16).astype(np.float64).reshape(n // 32, 32, m)
    top = np.abs(v).max(1)
    byte = np.clip(np.where(top > 0, np.frexp(top)[1] - 1 + 127 - 7, 1), 1, 254)
    codes = (v * np.exp2(127.0 - byte)[:, None, :]).reshape(n, m).astype(np.float32).astype(ml_dtypes.float8_e4m3fn).view(np.uint8)
    words = codes.reshape(n // 512, 128, 4, m).transpose(0, 1, 3, 2)
    return np.ascontiguousarray(words), np.ascontiguousarray(byte.astype(np.uint8).reshape(n // 512, 16, m))


def sigmoid(v):
    return 1.0 / (1.0 + np.exp(-np.maximum(v, -700.0)))


K, T, S, N = 1024, 2048, 512, 512


def setup_inputs():
    n = np.random.standard_normal
    s = mx_kscale(K)[:, None]
    packed_xT = pack_weight(n((K, T)) * s)
    packed_w1 = pack_weight(n((K, N)) / np.sqrt(2 * K) / s)
    packed_w2 = pack_weight(n((K, N)) / np.sqrt(2 * K) / s)
    packed_w3 = pack_weight(n((K, N)) / np.sqrt(2 * K) / s)
    packed_w4 = pack_weight(n((K, N)) / np.sqrt(2 * K) / s)
    return {
        "x_words": packed_xT[0],
        "x_scales": packed_xT[1],
        "eT": (n((K, S)) * s).astype(np.float32),
        "w1_words": packed_w1[0],
        "w1_scales": packed_w1[1],
        "w2_words": packed_w2[0],
        "w2_scales": packed_w2[1],
        "w3_words": packed_w3[0],
        "w3_scales": packed_w3[1],
        "w4_words": packed_w4[0],
        "w4_scales": packed_w4[1],
        "dec": (n((N, S))).astype(np.float32),
        "offs": striped(np.random.permutation(T)[:S]),
    }


def reference(x_words, x_scales, eT, w1_words, w1_scales, w2_words, w2_scales, w3_words, w3_scales, w4_words, w4_scales, dec, offs):
    eTq = mxq(f64(eT), 0, "e4m3")
    xq = unpack_weight(x_words, x_scales)[:, unstriped(offs)]
    g = sigmoid(unpack_weight(w1_words, w1_scales).T @ eTq + unpack_weight(w2_words, w2_scales).T @ xq)
    h = unpack_weight(w3_words, w3_scales).T @ eTq + unpack_weight(w4_words, w4_scales).T @ xq
    out_0 = f64(dec) * g + h
    return (out_0,) + planes(out_0)

@@ -1,0 +1,207 @@
+from contextlib import ExitStack
+
+import concourse.mybir as mybir
+
+K, T, S, N = 1024, 2048, 512, 512
+FLOPS = 4 * 2 * K * N * S
+
+F32 = mybir.dt.float32
+BF16 = mybir.dt.bfloat16
+I32 = mybir.dt.int32
+U32 = mybir.dt.uint32
+U16 = mybir.dt.uint16
+U8 = mybir.dt.uint8
+FP8X4 = mybir.dt.float8_e4m3fn_x4
+ACT = mybir.ActivationFunctionType
+ALU = mybir.AluOpType
+
+P = 128
+PACK = 4
+PASSES = K // (P * PACK)
+QUADS = 4
+QUAD = 32
+ROWS = 4
+HALF = S // 2
+LINE = 4
+E_SPLIT = 336
+Y_SPLIT = HALF + 176
+
+
+def tile_picked_zcft_sigmoid_po_kernel(
+    tc, x_words, x_scales, eT, w1_words, w1_scales, w2_words, w2_scales,
+    w3_words, w3_scales, w4_words, w4_scales, dec, offs, out_0, out_1, out_2,
+):
+    nc = tc.nc
+    with ExitStack() as ctx:
+        sb = ctx.enter_context(tc.tile_pool(name="sb", bufs=1))
+        ps = ctx.enter_context(tc.psum_pool(name="ps", bufs=1))
+
+        def sbuf(name, shape, dtype):
+            return sb.tile(shape, dtype, name=name, align_bytes=64)
+
+        offsets = sb.tile([P, S // 16], U16, name="offsets")
+        e_raw = [sbuf("e_raw%d" % o, [P, PACK, S], F32) for o in range(PASSES)]
+        e_bf = [sbuf("e_bf%d" % o, [P, S, PACK], BF16) for o in range(PASSES)]
+        e_codes = [sbuf("e_codes%d" % o, [P, S], U32) for o in range(PASSES)]
+        e_scales = [sbuf("e_scales%d" % o, [P, S], U8) for o in range(PASSES)]
+        x_table = [sbuf("x_table%d" % o, [P, T], U32) for o in range(PASSES)]
+        x_codes = [sbuf("x_codes%d" % o, [P, S], U32) for o in range(PASSES)]
+        xs_table = sbuf("xs_table", [P, T], U8)
+        xs_picked = sbuf("xs_picked", [P, S], U8)
+        w_raw = [sbuf("w_raw%d" % i, [P, PASSES, N], U32) for i in range(4)]
+        w_codes = [sbuf("w_codes%d" % i, [P, PACK, PASSES, P], U32) for i in range(4)]
+        ws_raw = [sbuf("ws_raw%d" % a, [P, PASSES, N], U8) for a in range(2)]
+        ws_rows = [sbuf("ws_rows%d" % a, [P, PASSES, N], U8) for a in range(2)]
+        ws_dealt = [sbuf("ws_dealt%d" % a, [P, PASSES, PACK, P], U8) for a in range(2)]
+        dec_sb = [sbuf("dec_sb%d" % t, [P, S], F32) for t in range(PACK)]
+        gate = [sbuf("gate%d" % t, [P, S], F32) for t in range(PACK)]
+        gated = sbuf("gated", [P, PACK, S], F32)
+        y = sbuf("y", [P, PACK, S], F32)
+        y_bf = sbuf("y_bf", [P, S, PACK], BF16)
+        y_codes = sbuf("y_codes", [P, S], U32)
+        y_scales = sbuf("y_scales", [P, S], U8)
+        g_ps = [ps.tile([P, S], F32, name="g_ps%d" % t) for t in range(PACK)]
+        h_ps = [[ps.tile([P, 2, HALF], F32, name="h_ps%d%d" % (c, u)) for u in range(2)] for c in range(2)]
+
+        w_words = [w1_words, w2_words, w3_words, w4_words]
+        w_scales = [w1_scales, w2_scales, w3_scales, w4_scales]
+        W1, W2, W3, W4 = 0, 1, 2, 3
+
+        def load_e(o):
+            rows = eT[o * P * PACK : (o + 1) * P * PACK, :]
+            nc.sync.dma_start(out=e_raw[o][:], in_=rows.rearrange("(p j) s -> p j s", j=PACK))
+
+        def load_x(o):
+            nc.sync.dma_start(out=x_table[o][:].bitcast(I32), in_=x_words[o].rearrange("p c r -> p (c r)").bitcast(I32))
+
+        def load_w(i):
+            nc.sync.dma_start(out=w_raw[i][:].bitcast(I32), in_=w_words[i].rearrange("o p c r -> p o (c r)").bitcast(I32))
+
+        def load_w_scales(i, queue):
+            first = ROWS * (i // 2)
+            rows = w_scales[i].bitcast(I32).rearrange("o (q r) c -> r q o c", r=ROWS)
+            for r in range(ROWS):
+                queue.dma_start(out=ws_raw[i % 2][:].bitcast(I32)[first + r : P : QUAD, :, :], in_=rows[r])
+
+        def load_x_scales():
+            for q in range(QUADS):
+                nc.gpsimd.dma_start(
+                    out=xs_table[:].bitcast(I32)[QUAD * q : QUAD * q + PASSES * ROWS, :],
+                    in_=x_scales.bitcast(I32)[:, ROWS * q : ROWS * (q + 1), :],
+                )
+
+        def round_interleaved(copy, dst, src, c0, c1):
+            copy(
+                out=dst[:, c0:c1, :].rearrange("p (c i) t -> p c t i", i=LINE),
+                in_=src[:, :, c0:c1].rearrange("p t (c i) -> p c t i", i=LINE),
+            )
+
+        def quantize(codes, scales, values, c0, c1):
+            nc.vector.quantize_mx(
+                out=codes[:, c0:c1].bitcast(FP8X4),
+                scales=scales[:, c0:c1],
+                in_=values[:, c0:c1, :].rearrange("p c t -> p (c t)"),
+            )
+
+        def deal_words(copy, i, t0, t1):
+            copy(
+                out=w_codes[i][:, t0:t1, :, :].rearrange("p t o (c i) -> p (o c) t i", i=LINE),
+                in_=w_raw[i][:].rearrange("p o (c i t) -> p (o c) t i", i=LINE, t=PACK)[:, :, t0:t1, :],
+            )
+
+        def deal_scales(a):
+            for q in range(QUADS):
+                live = slice(QUAD * q, QUAD * q + 2 * ROWS)
+                nc.scalar.copy(out=ws_rows[a][:].bitcast(U32)[live, :, :], in_=ws_raw[a][:].bitcast(U32)[live, :, :])
+            nc.vector.tensor_copy(out=ws_dealt[a][:], in_=ws_rows[a][:].rearrange("p o (m t) -> p o t m", t=PACK))
+
+        def product(out, i, o, t, c0, c1, start, stop):
+            if i % 2 == 0:
+                codes, scales = e_codes[o][:, c0:c1], e_scales[o][:, c0:c1]
+            else:
+                codes, scales = x_codes[o][:, c0:c1], xs_picked[ROWS * o : P, c0:c1]
+            nc.tensor.matmul_mx(
+                out=out,
+                lhsT=w_codes[i][:, t, o, :].bitcast(FP8X4),
+                lhsT_scale=ws_dealt[i % 2][ROWS * (i // 2) : P, o, t, :],
+                rhs=codes.bitcast(FP8X4),
+                rhs_scale=scales,
+                start=start,
+                stop=stop,
+            )
+
+        for plane in (xs_table, ws_rows[0], ws_rows[1]):
+            nc.vector.memset(plane[:].bitcast(I32), 0)
+
+        load_e(0)
+        load_x_scales()
+        load_w_scales(W1, nc.sync)
+        load_e(1)
+        load_w_scales(W3, nc.sync)
+        load_w(W1)
+        load_w(W3)
+        nc.sync.dma_start(offsets[:], offs)
+        load_w_scales(W2, nc.sync)
+        load_x(0)
+        load_w_scales(W4, nc.sync)
+        load_x(1)
+        load_w(W2)
+        load_w(W4)
+        dec_rows = dec.rearrange("(p t) s -> p t s", t=PACK)
+        for t in range(PACK):
+            nc.sync.dma_start(out=dec_sb[t][:], in_=dec_rows[:, t, :])
+
+        for o in range(PASSES):
+            round_interleaved(nc.vector.tensor_copy, e_bf[o], e_raw[o], 0, E_SPLIT)
+            round_interleaved(nc.scalar.copy, e_bf[o], e_raw[o], E_SPLIT, S)
+            quantize(e_codes[o], e_scales[o], e_bf[o], 0, S)
+        deal_scales(0)
+        for i in (W1, W3):
+            deal_words(nc.vector.tensor_copy, i, 0, 2)
+            deal_words(nc.scalar.copy, i, 2, PACK)
+
+        for o in range(PASSES):
+            for t in range(PACK):
+                product(g_ps[t][:], W1, o, t, 0, S, o == 0, False)
+        for o in range(PASSES):
+            for t in range(PACK):
+                for c in range(2):
+                    product(h_ps[c][t // 2][:, t % 2, :], W3, o, t, c * HALF, (c + 1) * HALF, o == 0 and t % 2 == 0, False)
+
+        nc.vector.tensor_copy(out=xs_picked[:], in_=xs_table[:].indirect(offsets[:]))
+        nc.vector.tensor_copy(out=x_codes[0][:], in_=x_table[0][:].indirect(offsets[:]))
+        deal_scales(1)
+        nc.vector.tensor_copy(out=x_codes[1][:], in_=x_table[1][:].indirect(offsets[:]))
+        deal_words(nc.vector.tensor_copy, W2, 0, 2)
+        deal_words(nc.scalar.copy, W2, 2, PACK)
+        deal_words(nc.vector.tensor_copy, W4, 0, PACK)
+
+        for t in range(PACK):
+            for o in range(PASSES):
+                product(g_ps[t][:], W2, o, t, 0, S, False, o == PASSES - 1)
+            nc.scalar.activation(out=gate[t][:], in_=g_ps[t][:], func=ACT.Sigmoid)
+            nc.vector.tensor_tensor(out=gated[:, t, :], in0=gate[t][:], in1=dec_sb[t][:], op=ALU.mult)
+
+        out_rows = out_0.rearrange("(p t) s -> p t s", t=PACK)
+        out_words = out_1[0].rearrange("p c r -> p (c r)").bitcast(I32)
+        for c in range(2):
+            c0, c1 = c * HALF, (c + 1) * HALF
+            for u in range(2):
+                for t in (2 * u, 2 * u + 1):
+                    for o in range(PASSES):
+                        product(h_ps[c][u][:, t % 2, :], W4, o, t, c0, c1, False, o == PASSES - 1 and t % 2 == 1)
+                pair = slice(2 * u, 2 * u + 2)
+                nc.vector.tensor_tensor(out=y[:, pair, c0:c1], in0=h_ps[c][u][:], in1=gated[:, pair, c0:c1], op=ALU.add)
+                nc.sync.dma_start(out=out_rows[:, pair, c0:c1], in_=y[:, pair, c0:c1])
+        round_interleaved(nc.scalar.copy, y_bf, y, 0, HALF)
+        round_interleaved(nc.vector.tensor_copy, y_bf, y, HALF, Y_SPLIT)
+        round_interleaved(nc.scalar.copy, y_bf, y, Y_SPLIT, S)
+        for c in range(2):
+            c0, c1 = c * HALF, (c + 1) * HALF
+            quantize(y_codes, y_scales, y_bf, c0, c1)
+            nc.sync.dma_start(out=out_words[:, c0:c1], in_=y_codes[:].bitcast(I32)[:, c0:c1])
+        for q in range(QUADS):
+            nc.scalar.dma_start(
+                out=out_2[0].bitcast(I32)[ROWS * q : ROWS * (q + 1), :],
+                in_=y_scales[:].bitcast(I32)[QUAD * q : QUAD * q + ROWS, :],
+            )

@@ -23,7 +23,6 @@ QUAD = 32
 ROWS = 4
 HALF = S // 2
 LINE = 4
-E_SPLIT = 336
 Y_SPLIT = HALF + 176
 
 
@@ -37,7 +36,7 @@ def tile_picked_zcft_sigmoid_po_kernel(
         ps = ctx.enter_context(tc.psum_pool(name="ps", bufs=1))
 
         def sbuf(name, shape, dtype):
-            return sb.tile(shape, dtype, name=name, align_bytes=64)
+            return sb.tile(shape, dtype, name=name, tag=name, align_bytes=64)
 
         offsets = sb.tile([P, S // 16], U16, name="offsets")
         e_raw = [sbuf("e_raw%d" % o, [P, PACK, S], F32) for o in range(PASSES)]
@@ -50,9 +49,9 @@ def tile_picked_zcft_sigmoid_po_kernel(
         xs_picked = sbuf("xs_picked", [P, S], U8)
         w_raw = [sbuf("w_raw%d" % i, [P, PASSES, N], U32) for i in range(4)]
         w_codes = [sbuf("w_codes%d" % i, [P, PACK, PASSES, P], U32) for i in range(4)]
-        ws_raw = [sbuf("ws_raw%d" % a, [P, PASSES, N], U8) for a in range(2)]
-        ws_rows = [sbuf("ws_rows%d" % a, [P, PASSES, N], U8) for a in range(2)]
-        ws_dealt = [sbuf("ws_dealt%d" % a, [P, PASSES, PACK, P], U8) for a in range(2)]
+        ws_stage = sbuf("ws_stage", [QUAD, ROWS, 4, N], U8)
+        ws_rows = sbuf("ws_rows", [P, 4, N], U8)
+        ws_dealt = {}
         dec_sb = [sbuf("dec_sb%d" % t, [P, S], F32) for t in range(PACK)]
         gate = [sbuf("gate%d" % t, [P, S], F32) for t in range(PACK)]
         gated = sbuf("gated", [P, PACK, S], F32)
@@ -74,14 +73,26 @@ def tile_picked_zcft_sigmoid_po_kernel(
         def load_x(o):
             nc.sync.dma_start(out=x_table[o][:].bitcast(I32), in_=x_words[o].rearrange("p c r -> p (c r)").bitcast(I32))
 
-        def load_w(i):
-            nc.sync.dma_start(out=w_raw[i][:].bitcast(I32), in_=w_words[i].rearrange("o p c r -> p o (c r)").bitcast(I32))
+        def load_w(i, o0, o1):
+            nc.sync.dma_start(
+                out=w_raw[i][:].bitcast(I32)[:, o0:o1, :],
+                in_=w_words[i].rearrange("o p c r -> p o (c r)").bitcast(I32)[:, o0:o1, :],
+            )
 
-        def load_w_scales(i, queue):
-            first = ROWS * (i // 2)
-            rows = w_scales[i].bitcast(I32).rearrange("o (q r) c -> r q o c", r=ROWS)
-            for r in range(ROWS):
-                queue.dma_start(out=ws_raw[i % 2][:].bitcast(I32)[first + r : P : QUAD, :, :], in_=rows[r])
+        def load_w_scales(i):
+            nc.scalar.dma_start(
+                out=ws_stage[:].bitcast(I32)[0:QUAD:ROWS, :, i, :],
+                in_=w_scales[i].bitcast(I32).rearrange("o (q r) c -> (o q) r c", r=ROWS),
+            )
+
+        def place_w_scales():
+            staged = ws_stage[:].rearrange("p r i c -> p r (i c)").bitcast(I32)
+            placed = ws_rows[:].rearrange("p i c -> p (i c)").bitcast(I32)
+            for q in range(QUADS):
+                nc.gpsimd.dma_start(
+                    out=placed[QUAD * q : QUAD * q + PASSES * ROWS, :],
+                    in_=staged[ROWS * q : QUAD : ROWS * QUADS, :, :],
+                )
 
         def load_x_scales():
             for q in range(QUADS):
@@ -103,17 +114,15 @@ def tile_picked_zcft_sigmoid_po_kernel(
                 in_=values[:, c0:c1, :].rearrange("p c t -> p (c t)"),
             )
 
-        def deal_words(copy, i, t0, t1):
-            copy(
-                out=w_codes[i][:, t0:t1, :, :].rearrange("p t o (c i) -> p (o c) t i", i=LINE),
-                in_=w_raw[i][:].rearrange("p o (c i t) -> p (o c) t i", i=LINE, t=PACK)[:, :, t0:t1, :],
+        def deal_words(i, o0, o1, t0, t1):
+            nc.vector.tensor_copy(
+                out=w_codes[i][:, t0:t1, o0:o1, :].rearrange("p t o (c i) -> p (o c) t i", i=LINE),
+                in_=w_raw[i][:, o0:o1, :].rearrange("p o (c i t) -> p (o c) t i", i=LINE, t=PACK)[:, :, t0:t1, :],
             )
 
-        def deal_scales(a):
-            for q in range(QUADS):
-                live = slice(QUAD * q, QUAD * q + 2 * ROWS)
-                nc.scalar.copy(out=ws_rows[a][:].bitcast(U32)[live, :, :], in_=ws_raw[a][:].bitcast(U32)[live, :, :])
-            nc.vector.tensor_copy(out=ws_dealt[a][:], in_=ws_rows[a][:].rearrange("p o (m t) -> p o t m", t=PACK))
+        def deal_scales(i, tag):
+            ws_dealt[i] = sb.tile([P, PACK, P], U8, name="ws_dealt%d" % i, tag=tag, align_bytes=64)
+            nc.vector.tensor_copy(out=ws_dealt[i][:], in_=ws_rows[:, i, :].rearrange("p (m t) -> p t m", t=PACK))
 
         def product(out, i, o, t, c0, c1, start, stop):
             if i % 2 == 0:
@@ -123,58 +132,60 @@ def tile_picked_zcft_sigmoid_po_kernel(
             nc.tensor.matmul_mx(
                 out=out,
                 lhsT=w_codes[i][:, t, o, :].bitcast(FP8X4),
-                lhsT_scale=ws_dealt[i % 2][ROWS * (i // 2) : P, o, t, :],
+                lhsT_scale=ws_dealt[i][ROWS * o : P, t, :],
                 rhs=codes.bitcast(FP8X4),
                 rhs_scale=scales,
                 start=start,
                 stop=stop,
             )
 
-        for plane in (xs_table, ws_rows[0], ws_rows[1]):
-            nc.vector.memset(plane[:].bitcast(I32), 0)
+        nc.gpsimd.memset(xs_table[:].bitcast(I32), 0)
+        nc.vector.memset(ws_rows[:].bitcast(I32), 0)
 
         load_e(0)
+        for i in range(4):
+            load_w_scales(i)
         load_x_scales()
-        load_w_scales(W1, nc.sync)
+        place_w_scales()
         load_e(1)
-        load_w_scales(W3, nc.sync)
-        load_w(W1)
-        load_w(W3)
+        load_w(W1, 0, PASSES)
         nc.sync.dma_start(offsets[:], offs)
-        load_w_scales(W2, nc.sync)
+        load_w(W3, 0, 1)
         load_x(0)
-        load_w_scales(W4, nc.sync)
         load_x(1)
-        load_w(W2)
-        load_w(W4)
+        load_w(W2, 0, PASSES)
+        load_w(W3, 1, PASSES)
+        load_w(W4, 0, PASSES)
         dec_rows = dec.rearrange("(p t) s -> p t s", t=PACK)
         for t in range(PACK):
             nc.sync.dma_start(out=dec_sb[t][:], in_=dec_rows[:, t, :])
 
         for o in range(PASSES):
-            round_interleaved(nc.vector.tensor_copy, e_bf[o], e_raw[o], 0, E_SPLIT)
-            round_interleaved(nc.scalar.copy, e_bf[o], e_raw[o], E_SPLIT, S)
-            quantize(e_codes[o], e_scales[o], e_bf[o], 0, S)
-        deal_scales(0)
-        for i in (W1, W3):
-            deal_words(nc.vector.tensor_copy, i, 0, 2)
-            deal_words(nc.scalar.copy, i, 2, PACK)
-
-        for o in range(PASSES):
-            for t in range(PACK):
-                product(g_ps[t][:], W1, o, t, 0, S, o == 0, False)
-        for o in range(PASSES):
-            for t in range(PACK):
-                for c in range(2):
-                    product(h_ps[c][t // 2][:, t % 2, :], W3, o, t, c * HALF, (c + 1) * HALF, o == 0 and t % 2 == 0, False)
-
+            round_interleaved(nc.scalar.copy, e_bf[o], e_raw[o], 0, S)
+        quantize(e_codes[0], e_scales[0], e_bf[0], 0, S)
+        deal_words(W1, 0, PASSES, 0, PACK)
         nc.vector.tensor_copy(out=xs_picked[:], in_=xs_table[:].indirect(offsets[:]))
+        deal_words(W3, 0, 1, 0, PACK)
+        deal_scales(W1, "xs_table")
+        deal_scales(W3, "ws_dealt3")
+        quantize(e_codes[1], e_scales[1], e_bf[1], 0, S)
+
+        for t in range(PACK):
+            product(g_ps[t][:], W1, 0, t, 0, S, True, False)
+        for t in range(PACK):
+            for c in range(2):
+                product(h_ps[c][t // 2][:, t % 2, :], W3, 0, t, c * HALF, (c + 1) * HALF, t % 2 == 0, False)
+        for t in range(PACK):
+            product(g_ps[t][:], W1, 1, t, 0, S, False, False)
+
         nc.vector.tensor_copy(out=x_codes[0][:], in_=x_table[0][:].indirect(offsets[:]))
-        deal_scales(1)
+        deal_scales(W2, "ws_dealt2")
+        deal_scales(W4, "ws_dealt4")
         nc.vector.tensor_copy(out=x_codes[1][:], in_=x_table[1][:].indirect(offsets[:]))
-        deal_words(nc.vector.tensor_copy, W2, 0, 2)
-        deal_words(nc.scalar.copy, W2, 2, PACK)
-        deal_words(nc.vector.tensor_copy, W4, 0, PACK)
+        deal_words(W2, 0, PASSES, 0, 2)
+        deal_words(W2, 0, PASSES, 2, PACK)
+        deal_words(W3, 1, PASSES, 0, PACK)
+        deal_words(W4, 0, PASSES, 0, PACK)
 
         for t in range(PACK):
             for o in range(PASSES):
@@ -188,6 +199,7 @@ def tile_picked_zcft_sigmoid_po_kernel(
             c0, c1 = c * HALF, (c + 1) * HALF
             for u in range(2):
                 for t in (2 * u, 2 * u + 1):
+                    product(h_ps[c][u][:, t % 2, :], W3, 1, t, c0, c1, False, False)
                     for o in range(PASSES):
                         product(h_ps[c][u][:, t % 2, :], W4, o, t, c0, c1, False, o == PASSES - 1 and t % 2 == 1)
                 pair = slice(2 * u, 2 * u + 2)
@@ -201,7 +213,7 @@ def tile_picked_zcft_sigmoid_po_kernel(
             quantize(y_codes, y_scales, y_bf, c0, c1)
             nc.sync.dma_start(out=out_words[:, c0:c1], in_=y_codes[:].bitcast(I32)[:, c0:c1])
         for q in range(QUADS):
-            nc.scalar.dma_start(
+            (nc.scalar, nc.sync)[q % 2].dma_start(
                 out=out_2[0].bitcast(I32)[ROWS * q : ROWS * (q + 1), :],
                 in_=y_scales[:].bitcast(I32)[QUAD * q : QUAD * q + ROWS, :],
             )

@@ -23,6 +23,7 @@ QUAD = 32
 ROWS = 4
 HALF = S // 2
 LINE = 4
+E_SPLIT = 336
 Y_SPLIT = HALF + 176
 
 
@@ -46,12 +47,11 @@ def tile_picked_zcft_sigmoid_po_kernel(
         x_table = [sbuf("x_table%d" % o, [P, T], U32) for o in range(PASSES)]
         x_codes = [sbuf("x_codes%d" % o, [P, S], U32) for o in range(PASSES)]
         xs_table = sbuf("xs_table", [P, T], U8)
-        xs_picked = sbuf("xs_picked", [P, S], U8)
         w_raw = [sbuf("w_raw%d" % i, [P, PASSES, N], U32) for i in range(4)]
         w_codes = [sbuf("w_codes%d" % i, [P, PACK, PASSES, P], U32) for i in range(4)]
-        ws_stage = sbuf("ws_stage", [QUAD, ROWS, 4, N], U8)
-        ws_rows = sbuf("ws_rows", [P, 4, N], U8)
-        ws_dealt = {}
+        ws_raw = [sbuf("ws_raw%d" % a, [P, PASSES, N], U8) for a in range(2)]
+        ws_early = sbuf("ws_early", [P, PASSES, N], U8)
+        ws_dealt = [sbuf("ws_dealt%d" % a, [P, PASSES, PACK, P], U8) for a in range(2)]
         dec_sb = [sbuf("dec_sb%d" % t, [P, S], F32) for t in range(PACK)]
         gate = [sbuf("gate%d" % t, [P, S], F32) for t in range(PACK)]
         gated = sbuf("gated", [P, PACK, S], F32)
@@ -79,20 +79,11 @@ def tile_picked_zcft_sigmoid_po_kernel(
                 in_=w_words[i].rearrange("o p c r -> p o (c r)").bitcast(I32)[:, o0:o1, :],
             )
 
-        def load_w_scales(i):
-            nc.scalar.dma_start(
-                out=ws_stage[:].bitcast(I32)[0:QUAD:ROWS, :, i, :],
-                in_=w_scales[i].bitcast(I32).rearrange("o (q r) c -> (o q) r c", r=ROWS),
-            )
-
-        def place_w_scales():
-            staged = ws_stage[:].rearrange("p r i c -> p r (i c)").bitcast(I32)
-            placed = ws_rows[:].rearrange("p i c -> p (i c)").bitcast(I32)
-            for q in range(QUADS):
-                nc.gpsimd.dma_start(
-                    out=placed[QUAD * q : QUAD * q + PASSES * ROWS, :],
-                    in_=staged[ROWS * q : QUAD : ROWS * QUADS, :, :],
-                )
+        def load_w_scales(i, tile, r0, r1):
+            first = ROWS * (i // 2)
+            rows = w_scales[i].bitcast(I32).rearrange("o (q r) c -> r q o c", r=ROWS)
+            for r in range(r0, r1):
+                nc.sync.dma_start(out=tile[:].bitcast(I32)[first + r : P : QUAD, :, :], in_=rows[r])
 
         def load_x_scales():
             for q in range(QUADS):
@@ -114,15 +105,14 @@ def tile_picked_zcft_sigmoid_po_kernel(
                 in_=values[:, c0:c1, :].rearrange("p c t -> p (c t)"),
             )
 
-        def deal_words(i, o0, o1, t0, t1):
-            nc.vector.tensor_copy(
+        def deal_words(copy, i, o0, o1, t0, t1):
+            copy(
                 out=w_codes[i][:, t0:t1, o0:o1, :].rearrange("p t o (c i) -> p (o c) t i", i=LINE),
                 in_=w_raw[i][:, o0:o1, :].rearrange("p o (c i t) -> p (o c) t i", i=LINE, t=PACK)[:, :, t0:t1, :],
             )
 
-        def deal_scales(i, tag):
-            ws_dealt[i] = sb.tile([P, PACK, P], U8, name="ws_dealt%d" % i, tag=tag, align_bytes=64)
-            nc.vector.tensor_copy(out=ws_dealt[i][:], in_=ws_rows[:, i, :].rearrange("p (m t) -> p t m", t=PACK))
+        def deal_scales(a):
+            nc.vector.tensor_copy(out=ws_dealt[a][:], in_=ws_raw[a][:].rearrange("p o (m t) -> p o t m", t=PACK))
 
         def product(out, i, o, t, c0, c1, start, stop):
             if i % 2 == 0:
@@ -132,60 +122,66 @@ def tile_picked_zcft_sigmoid_po_kernel(
             nc.tensor.matmul_mx(
                 out=out,
                 lhsT=w_codes[i][:, t, o, :].bitcast(FP8X4),
-                lhsT_scale=ws_dealt[i][ROWS * o : P, t, :],
+                lhsT_scale=ws_dealt[i % 2][ROWS * (i // 2) : P, o, t, :],
                 rhs=codes.bitcast(FP8X4),
                 rhs_scale=scales,
                 start=start,
                 stop=stop,
             )
 
-        nc.gpsimd.memset(xs_table[:].bitcast(I32), 0)
-        nc.vector.memset(ws_rows[:].bitcast(I32), 0)
+        for plane in (xs_table, ws_raw[1], ws_raw[0]):
+            nc.vector.memset(plane[:].bitcast(I32), 0)
 
-        load_e(0)
-        for i in range(4):
-            load_w_scales(i)
         load_x_scales()
-        place_w_scales()
-        load_e(1)
+        load_w_scales(W1, ws_early, 0, 3)
+        load_e(0)
+        load_w_scales(W1, ws_early, 3, ROWS)
+        load_w_scales(W3, ws_early, 0, ROWS)
         load_w(W1, 0, PASSES)
+        load_e(1)
         nc.sync.dma_start(offsets[:], offs)
-        load_w(W3, 0, 1)
+        load_w_scales(W2, ws_raw[1], 0, ROWS)
         load_x(0)
+        load_w_scales(W4, ws_raw[1], 0, ROWS)
+        load_w(W3, 0, PASSES)
         load_x(1)
         load_w(W2, 0, PASSES)
-        load_w(W3, 1, PASSES)
         load_w(W4, 0, PASSES)
         dec_rows = dec.rearrange("(p t) s -> p t s", t=PACK)
         for t in range(PACK):
             nc.sync.dma_start(out=dec_sb[t][:], in_=dec_rows[:, t, :])
 
-        for o in range(PASSES):
-            round_interleaved(nc.scalar.copy, e_bf[o], e_raw[o], 0, S)
+        round_interleaved(nc.vector.tensor_copy, e_bf[0], e_raw[0], 0, E_SPLIT)
+        round_interleaved(nc.scalar.copy, e_bf[0], e_raw[0], E_SPLIT, S)
         quantize(e_codes[0], e_scales[0], e_bf[0], 0, S)
-        deal_words(W1, 0, PASSES, 0, PACK)
-        nc.vector.tensor_copy(out=xs_picked[:], in_=xs_table[:].indirect(offsets[:]))
-        deal_words(W3, 0, 1, 0, PACK)
-        deal_scales(W1, "xs_table")
-        deal_scales(W3, "ws_dealt3")
+        for q in range(QUADS):
+            live = slice(QUAD * q, QUAD * q + 2 * ROWS)
+            nc.scalar.copy(out=ws_raw[0][:].bitcast(U32)[live, :, :], in_=ws_early[:].bitcast(U32)[live, :, :])
+        deal_scales(0)
+        deal_words(nc.vector.tensor_copy, W1, 0, PASSES, 0, 2)
+        deal_words(nc.scalar.copy, W1, 0, PASSES, 2, PACK)
+        round_interleaved(nc.vector.tensor_copy, e_bf[1], e_raw[1], 0, E_SPLIT)
+        round_interleaved(nc.scalar.copy, e_bf[1], e_raw[1], E_SPLIT, S)
         quantize(e_codes[1], e_scales[1], e_bf[1], 0, S)
-
-        for t in range(PACK):
-            product(g_ps[t][:], W1, 0, t, 0, S, True, False)
-        for t in range(PACK):
-            for c in range(2):
-                product(h_ps[c][t // 2][:, t % 2, :], W3, 0, t, c * HALF, (c + 1) * HALF, t % 2 == 0, False)
-        for t in range(PACK):
-            product(g_ps[t][:], W1, 1, t, 0, S, False, False)
+        for o in range(PASSES):
+            for t in range(PACK):
+                product(g_ps[t][:], W1, o, t, 0, S, o == 0, False)
 
         nc.vector.tensor_copy(out=x_codes[0][:], in_=x_table[0][:].indirect(offsets[:]))
-        deal_scales(W2, "ws_dealt2")
-        deal_scales(W4, "ws_dealt4")
+        xs_picked = sb.tile([P, S], U8, name="xs_picked", tag="x_table0", align_bytes=64)
+        nc.vector.tensor_copy(out=xs_picked[:], in_=xs_table[:].indirect(offsets[:]))
+        deal_words(nc.scalar.copy, W3, 0, PASSES, 0, 2)
+        deal_words(nc.scalar.copy, W3, 0, PASSES, 2, PACK)
+        for o in range(PASSES):
+            for t in range(PACK):
+                for c in range(2):
+                    product(h_ps[c][t // 2][:, t % 2, :], W3, o, t, c * HALF, (c + 1) * HALF, o == 0 and t % 2 == 0, False)
+
+        deal_scales(1)
         nc.vector.tensor_copy(out=x_codes[1][:], in_=x_table[1][:].indirect(offsets[:]))
-        deal_words(W2, 0, PASSES, 0, 2)
-        deal_words(W2, 0, PASSES, 2, PACK)
-        deal_words(W3, 1, PASSES, 0, PACK)
-        deal_words(W4, 0, PASSES, 0, PACK)
+        deal_words(nc.vector.tensor_copy, W2, 0, PASSES, 0, 2)
+        deal_words(nc.vector.tensor_copy, W2, 0, PASSES, 2, PACK)
+        deal_words(nc.vector.tensor_copy, W4, 0, PASSES, 0, PACK)
 
         for t in range(PACK):
             for o in range(PASSES):
@@ -199,7 +195,6 @@ def tile_picked_zcft_sigmoid_po_kernel(
             c0, c1 = c * HALF, (c + 1) * HALF
             for u in range(2):
                 for t in (2 * u, 2 * u + 1):
-                    product(h_ps[c][u][:, t % 2, :], W3, 1, t, c0, c1, False, False)
                     for o in range(PASSES):
                         product(h_ps[c][u][:, t % 2, :], W4, o, t, c0, c1, False, o == PASSES - 1 and t % 2 == 1)
                 pair = slice(2 * u, 2 * u + 2)

@@ -24,7 +24,6 @@ ROWS = 4
 HALF = S // 2
 LINE = 4
 E_SPLIT = 336
-Y_SPLIT = HALF + 176
 
 
 def tile_picked_zcft_sigmoid_po_kernel(
@@ -133,9 +132,9 @@ def tile_picked_zcft_sigmoid_po_kernel(
             nc.vector.memset(plane[:].bitcast(I32), 0)
 
         load_x_scales()
-        load_w_scales(W1, ws_early, 0, 3)
+        load_w_scales(W1, ws_early, 0, 2)
         load_e(0)
-        load_w_scales(W1, ws_early, 3, ROWS)
+        load_w_scales(W1, ws_early, 2, ROWS)
         load_w_scales(W3, ws_early, 0, ROWS)
         load_w(W1, 0, PASSES)
         load_e(1)
@@ -187,13 +186,14 @@ def tile_picked_zcft_sigmoid_po_kernel(
             for o in range(PASSES):
                 product(g_ps[t][:], W2, o, t, 0, S, False, o == PASSES - 1)
             nc.scalar.activation(out=gate[t][:], in_=g_ps[t][:], func=ACT.Sigmoid)
-            nc.vector.tensor_tensor(out=gated[:, t, :], in0=gate[t][:], in1=dec_sb[t][:], op=ALU.mult)
+            engine = nc.gpsimd if t == PACK - 1 else nc.vector
+            engine.tensor_tensor(out=gated[:, t, :], in0=gate[t][:], in1=dec_sb[t][:], op=ALU.mult)
 
         out_rows = out_0.rearrange("(p t) s -> p t s", t=PACK)
         out_words = out_1[0].rearrange("p c r -> p (c r)").bitcast(I32)
-        for c in range(2):
-            c0, c1 = c * HALF, (c + 1) * HALF
-            for u in range(2):
+        for u in range(2):
+            for c in range(2):
+                c0, c1 = c * HALF, (c + 1) * HALF
                 for t in (2 * u, 2 * u + 1):
                     for o in range(PASSES):
                         product(h_ps[c][u][:, t % 2, :], W4, o, t, c0, c1, False, o == PASSES - 1 and t % 2 == 1)
@@ -201,8 +201,7 @@ def tile_picked_zcft_sigmoid_po_kernel(
                 nc.vector.tensor_tensor(out=y[:, pair, c0:c1], in0=h_ps[c][u][:], in1=gated[:, pair, c0:c1], op=ALU.add)
                 nc.sync.dma_start(out=out_rows[:, pair, c0:c1], in_=y[:, pair, c0:c1])
         round_interleaved(nc.scalar.copy, y_bf, y, 0, HALF)
-        round_interleaved(nc.vector.tensor_copy, y_bf, y, HALF, Y_SPLIT)
-        round_interleaved(nc.scalar.copy, y_bf, y, Y_SPLIT, S)
+        round_interleaved(nc.vector.tensor_copy, y_bf, y, HALF, S)
         for c in range(2):
             c0, c1 = c * HALF, (c + 1) * HALF
             quantize(y_codes, y_scales, y_bf, c0, c1)

from contextlib import ExitStack

import concourse.mybir as mybir

K, T, S, N = 1024, 2048, 512, 512
FLOPS = 4 * 2 * K * N * S

F32 = mybir.dt.float32
BF16 = mybir.dt.bfloat16
I32 = mybir.dt.int32
U32 = mybir.dt.uint32
U16 = mybir.dt.uint16
U8 = mybir.dt.uint8
FP8X4 = mybir.dt.float8_e4m3fn_x4
ACT = mybir.ActivationFunctionType
ALU = mybir.AluOpType

P = 128
PACK = 4
PASSES = K // (P * PACK)
QUADS = 4
QUAD = 32
ROWS = 4
HALF = S // 2
LINE = 4
E_SPLIT = 336


def tile_picked_zcft_sigmoid_po_kernel(
    tc, x_words, x_scales, eT, w1_words, w1_scales, w2_words, w2_scales,
    w3_words, w3_scales, w4_words, w4_scales, dec, offs, out_0, out_1, out_2,
):
    nc = tc.nc
    with ExitStack() as ctx:
        sb = ctx.enter_context(tc.tile_pool(name="sb", bufs=1))
        ps = ctx.enter_context(tc.psum_pool(name="ps", bufs=1))

        def sbuf(name, shape, dtype):
            return sb.tile(shape, dtype, name=name, tag=name, align_bytes=64)

        offsets = sb.tile([P, S // 16], U16, name="offsets")
        e_raw = [sbuf("e_raw%d" % o, [P, PACK, S], F32) for o in range(PASSES)]
        e_bf = [sbuf("e_bf%d" % o, [P, S, PACK], BF16) for o in range(PASSES)]
        e_codes = [sbuf("e_codes%d" % o, [P, S], U32) for o in range(PASSES)]
        e_scales = [sbuf("e_scales%d" % o, [P, S], U8) for o in range(PASSES)]
        x_table = [sbuf("x_table%d" % o, [P, T], U32) for o in range(PASSES)]
        x_codes = [sbuf("x_codes%d" % o, [P, S], U32) for o in range(PASSES)]
        xs_table = sbuf("xs_table", [P, T], U8)
        w_raw = [sbuf("w_raw%d" % i, [P, PASSES, N], U32) for i in range(4)]
        w_codes = [sbuf("w_codes%d" % i, [P, PACK, PASSES, P], U32) for i in range(4)]
        ws_raw = [sbuf("ws_raw%d" % a, [P, PASSES, N], U8) for a in range(2)]
        ws_early = sbuf("ws_early", [P, PASSES, N], U8)
        ws_dealt = [sbuf("ws_dealt%d" % a, [P, PASSES, PACK, P], U8) for a in range(2)]
        dec_sb = [sbuf("dec_sb%d" % t, [P, S], F32) for t in range(PACK)]
        gate = [sbuf("gate%d" % t, [P, S], F32) for t in range(PACK)]
        gated = sbuf("gated", [P, PACK, S], F32)
        y = sbuf("y", [P, PACK, S], F32)
        y_bf = sbuf("y_bf", [P, S, PACK], BF16)
        y_codes = sbuf("y_codes", [P, S], U32)
        y_scales = sbuf("y_scales", [P, S], U8)
        g_ps = [ps.tile([P, S], F32, name="g_ps%d" % t) for t in range(PACK)]
        h_ps = [[ps.tile([P, 2, HALF], F32, name="h_ps%d%d" % (c, u)) for u in range(2)] for c in range(2)]

        w_words = [w1_words, w2_words, w3_words, w4_words]
        w_scales = [w1_scales, w2_scales, w3_scales, w4_scales]
        W1, W2, W3, W4 = 0, 1, 2, 3

        def load_e(o):
            rows = eT[o * P * PACK : (o + 1) * P * PACK, :]
            nc.sync.dma_start(out=e_raw[o][:], in_=rows.rearrange("(p j) s -> p j s", j=PACK))

        def load_x(o):
            nc.sync.dma_start(out=x_table[o][:].bitcast(I32), in_=x_words[o].rearrange("p c r -> p (c r)").bitcast(I32))

        def load_w(i, o0, o1):
            nc.sync.dma_start(
                out=w_raw[i][:].bitcast(I32)[:, o0:o1, :],
                in_=w_words[i].rearrange("o p c r -> p o (c r)").bitcast(I32)[:, o0:o1, :],
            )

        def load_w_scales(i, tile, r0, r1):
            first = ROWS * (i // 2)
            rows = w_scales[i].bitcast(I32).rearrange("o (q r) c -> r q o c", r=ROWS)
            for r in range(r0, r1):
                nc.sync.dma_start(out=tile[:].bitcast(I32)[first + r : P : QUAD, :, :], in_=rows[r])

        def load_x_scales():
            for q in range(QUADS):
                nc.gpsimd.dma_start(
                    out=xs_table[:].bitcast(I32)[QUAD * q : QUAD * q + PASSES * ROWS, :],
                    in_=x_scales.bitcast(I32)[:, ROWS * q : ROWS * (q + 1), :],
                )

        def round_interleaved(copy, dst, src, c0, c1):
            copy(
                out=dst[:, c0:c1, :].rearrange("p (c i) t -> p c t i", i=LINE),
                in_=src[:, :, c0:c1].rearrange("p t (c i) -> p c t i", i=LINE),
            )

        def quantize(codes, scales, values, c0, c1):
            nc.vector.quantize_mx(
                out=codes[:, c0:c1].bitcast(FP8X4),
                scales=scales[:, c0:c1],
                in_=values[:, c0:c1, :].rearrange("p c t -> p (c t)"),
            )

        def deal_words(copy, i, o0, o1, t0, t1):
            copy(
                out=w_codes[i][:, t0:t1, o0:o1, :].rearrange("p t o (c i) -> p (o c) t i", i=LINE),
                in_=w_raw[i][:, o0:o1, :].rearrange("p o (c i t) -> p (o c) t i", i=LINE, t=PACK)[:, :, t0:t1, :],
            )

        def deal_scales(a):
            nc.vector.tensor_copy(out=ws_dealt[a][:], in_=ws_raw[a][:].rearrange("p o (m t) -> p o t m", t=PACK))

        def product(out, i, o, t, c0, c1, start, stop):
            if i % 2 == 0:
                codes, scales = e_codes[o][:, c0:c1], e_scales[o][:, c0:c1]
            else:
                codes, scales = x_codes[o][:, c0:c1], xs_picked[ROWS * o : P, c0:c1]
            nc.tensor.matmul_mx(
                out=out,
                lhsT=w_codes[i][:, t, o, :].bitcast(FP8X4),
                lhsT_scale=ws_dealt[i % 2][ROWS * (i // 2) : P, o, t, :],
                rhs=codes.bitcast(FP8X4),
                rhs_scale=scales,
                start=start,
                stop=stop,
            )

        for plane in (xs_table, ws_raw[1], ws_raw[0]):
            nc.vector.memset(plane[:].bitcast(I32), 0)

        load_x_scales()
        load_w_scales(W1, ws_early, 0, 2)
        load_e(0)
        load_w_scales(W1, ws_early, 2, ROWS)
        load_w_scales(W3, ws_early, 0, ROWS)
        load_w(W1, 0, PASSES)
        load_e(1)
        nc.sync.dma_start(offsets[:], offs)
        load_w_scales(W2, ws_raw[1], 0, ROWS)
        load_x(0)
        load_w_scales(W4, ws_raw[1], 0, ROWS)
        load_w(W3, 0, PASSES)
        load_x(1)
        load_w(W2, 0, PASSES)
        load_w(W4, 0, PASSES)
        dec_rows = dec.rearrange("(p t) s -> p t s", t=PACK)
        for t in range(PACK):
            nc.sync.dma_start(out=dec_sb[t][:], in_=dec_rows[:, t, :])

        round_interleaved(nc.vector.tensor_copy, e_bf[0], e_raw[0], 0, E_SPLIT)
        round_interleaved(nc.scalar.copy, e_bf[0], e_raw[0], E_SPLIT, S)
        quantize(e_codes[0], e_scales[0], e_bf[0], 0, S)
        for q in range(QUADS):
            live = slice(QUAD * q, QUAD * q + 2 * ROWS)
            nc.scalar.copy(out=ws_raw[0][:].bitcast(U32)[live, :, :], in_=ws_early[:].bitcast(U32)[live, :, :])
        deal_scales(0)
        deal_words(nc.vector.tensor_copy, W1, 0, PASSES, 0, 2)
        deal_words(nc.scalar.copy, W1, 0, PASSES, 2, PACK)
        round_interleaved(nc.vector.tensor_copy, e_bf[1], e_raw[1], 0, E_SPLIT)
        round_interleaved(nc.scalar.copy, e_bf[1], e_raw[1], E_SPLIT, S)
        quantize(e_codes[1], e_scales[1], e_bf[1], 0, S)
        for o in range(PASSES):
            for t in range(PACK):
                product(g_ps[t][:], W1, o, t, 0, S, o == 0, False)

        nc.vector.tensor_copy(out=x_codes[0][:], in_=x_table[0][:].indirect(offsets[:]))
        xs_picked = sb.tile([P, S], U8, name="xs_picked", tag="x_table0", align_bytes=64)
        nc.vector.tensor_copy(out=xs_picked[:], in_=xs_table[:].indirect(offsets[:]))
        deal_words(nc.scalar.copy, W3, 0, PASSES, 0, 2)
        deal_words(nc.scalar.copy, W3, 0, PASSES, 2, PACK)
        for o in range(PASSES):
            for t in range(PACK):
                for c in range(2):
                    product(h_ps[c][t // 2][:, t % 2, :], W3, o, t, c * HALF, (c + 1) * HALF, o == 0 and t % 2 == 0, False)

        deal_scales(1)
        nc.vector.tensor_copy(out=x_codes[1][:], in_=x_table[1][:].indirect(offsets[:]))
        deal_words(nc.vector.tensor_copy, W2, 0, PASSES, 0, 2)
        deal_words(nc.vector.tensor_copy, W2, 0, PASSES, 2, PACK)
        deal_words(nc.vector.tensor_copy, W4, 0, PASSES, 0, PACK)

        for t in range(PACK):
            for o in range(PASSES):
                product(g_ps[t][:], W2, o, t, 0, S, False, o == PASSES - 1)
            nc.scalar.activation(out=gate[t][:], in_=g_ps[t][:], func=ACT.Sigmoid)
            engine = nc.gpsimd if t == PACK - 1 else nc.vector
            engine.tensor_tensor(out=gated[:, t, :], in0=gate[t][:], in1=dec_sb[t][:], op=ALU.mult)

        out_rows = out_0.rearrange("(p t) s -> p t s", t=PACK)
        out_words = out_1[0].rearrange("p c r -> p (c r)").bitcast(I32)
        for u in range(2):
            for c in range(2):
                c0, c1 = c * HALF, (c + 1) * HALF
                for t in (2 * u, 2 * u + 1):
                    for o in range(PASSES):
                        product(h_ps[c][u][:, t % 2, :], W4, o, t, c0, c1, False, o == PASSES - 1 and t % 2 == 1)
                pair = slice(2 * u, 2 * u + 2)
                nc.vector.tensor_tensor(out=y[:, pair, c0:c1], in0=h_ps[c][u][:], in1=gated[:, pair, c0:c1], op=ALU.add)
                nc.sync.dma_start(out=out_rows[:, pair, c0:c1], in_=y[:, pair, c0:c1])
        round_interleaved(nc.scalar.copy, y_bf, y, 0, HALF)
        round_interleaved(nc.vector.tensor_copy, y_bf, y, HALF, S)
        for c in range(2):
            c0, c1 = c * HALF, (c + 1) * HALF
            quantize(y_codes, y_scales, y_bf, c0, c1)
            nc.sync.dma_start(out=out_words[:, c0:c1], in_=y_codes[:].bitcast(I32)[:, c0:c1])
        for q in range(QUADS):
            (nc.scalar, nc.sync)[q % 2].dma_start(
                out=out_2[0].bitcast(I32)[ROWS * q : ROWS * (q + 1), :],
                in_=y_scales[:].bitcast(I32)[QUAD * q : QUAD * q + ROWS, :],
            )
